import numpy as np
import ml_dtypes


def mxq(x, axis, fmt="e4m3"):
    dtype, down = {"e4m3": (ml_dtypes.float8_e4m3fn, 7), "e5m2": (ml_dtypes.float8_e5m2, 14)}[fmt]
    v = np.moveaxis(np.asarray(x, np.float32).astype(ml_dtypes.bfloat16).astype(np.float64), axis, -1)
    blocks = v.reshape(v.shape[:-1] + (-1, 32))
    amax = np.abs(blocks).max(-1, keepdims=True)
    byte = np.maximum(np.where(amax > 0, np.frexp(amax)[1] - 1 + 127, 0) - down, 1)
    scale = np.exp2(byte - 127.0)
    codes = (blocks / scale).astype(np.float32).astype(dtype).astype(np.float64)
    return np.moveaxis((codes * scale).reshape(v.shape), -1, axis)


WIDE = False


def mx_kscale(k):
    if not WIDE:
        return np.ones(k)
    levels = np.array([10, -10, 5, -5, 0])
    if k % 512:
        return np.exp2(np.random.permutation(np.resize(levels, k // 32))).repeat(32)
    a = np.empty((k // 512, 16))
    for p in range(k // 512):
        a[p, :8] = np.random.permutation(np.resize(levels, 8))
        for g in range(8):
            far = levels[np.abs(levels - a[p, g]) >= 10]
            a[p, g + 8] = far[np.random.randint(len(far))]
    return np.exp2(a.ravel()).repeat(32)


def f64(x):
    return np.asarray(x).astype(np.float64)


def striped(idx):
    return np.tile(idx.reshape(-1, 16).T, (8, 1)).astype(np.uint16)


def unstriped(offs):
    return offs[:16].T.reshape(-1).astype(np.int64)


def pack_weight(w):
    k, n = w.shape
    w = f64(np.asarray(w, np.float32).astype(ml_dtypes.bfloat16)).reshape(k // 32, 32, n)
    amax = np.abs(w).max(1)
    byte = np.clip(np.where(amax > 0, np.frexp(amax)[1] - 1 + 127 - 7, 1), 1, 254)
    scaled = (w * np.exp2(127.0 - byte)[:, None, :]).reshape(k, n).astype(np.float32)
    words = np.ascontiguousarray(scaled.reshape(k // 512, 128, 4, n).transpose(0, 1, 3, 2)).astype(ml_dtypes.float8_e4m3fn).view(np.uint8)
    return words, np.ascontiguousarray(byte.astype(np.uint8).reshape(k // 512, 16, n))


def unpack_weight(words, scales):
    g, p, n, _ = words.shape
    vals = np.ascontiguousarray(words).view(ml_dtypes.float8_e4m3fn).astype(np.float64) * np.repeat(np.exp2(scales.astype(np.float64) - 127.0), 8, axis=1)[..., None]
    return vals.transpose(0, 1, 3, 2).reshape(g * 512, n)


def relu(v):
    return np.maximum(v, 0.0)


K, T, D, S, V, N = 512, 2048, 4, 512, 128, 256


def setup_inputs():
    n = np.random.standard_normal
    s = mx_kscale(K)[:, None]
    packed = pack_weight(n((K, T)) * s)
    return {
        "x_words": packed[0],
        "x_scales": packed[1],
        "w": (n((K, N)) / np.sqrt(K) / s).astype(np.float32),
        "b": (0.3 * n((N, 1))).astype(np.float32),
        "offs": striped(np.random.permutation(T)[:S]),
    }


def reference(x_words, x_scales, w, b, offs):
    idx = unstriped(offs)
    xq = unpack_weight(x_words, x_scales)[:, idx]
    y = mxq(f64(w), 0, "e4m3").T @ xq
    y = relu(y + f64(b))
    return y.reshape(N, V, D).max(axis=2)

@@ -1,0 +1,104 @@
+from contextlib import ExitStack
+
+import concourse.mybir as mybir
+
+K, T, D, S, V, N = 512, 2048, 4, 512, 128, 256
+FLOPS = 2 * K * N * S
+
+F32 = mybir.dt.float32
+BF16 = mybir.dt.bfloat16
+I32 = mybir.dt.int32
+U32 = mybir.dt.uint32
+U16 = mybir.dt.uint16
+U8 = mybir.dt.uint8
+FP8X4 = mybir.dt.float8_e4m3fn_x4
+RELU = mybir.ActivationFunctionType.Relu
+MAX = mybir.AluOpType.max
+AX_X = mybir.AxisListType.X
+
+P = 128
+PACK = 4
+HALVES = N // P
+CHUNK = 256
+CHUNKS = S // CHUNK
+LANES = 16
+
+
+def tile_picked_pool_lin_relu_sub_p_kernel(tc, x_words, x_scales, w, b, offs, out):
+    nc = tc.nc
+    with ExitStack() as ctx:
+        keep = ctx.enter_context(tc.tile_pool(name="keep", bufs=1))
+        psum = ctx.enter_context(tc.psum_pool(name="psum", bufs=1))
+
+        offsets = keep.tile([P, S // LANES], U16, name="offsets")
+        w_raw = keep.tile([P, PACK, N], F32, name="w_raw")
+        word_table = keep.tile([P, T], U32, name="word_table")
+        scale_table = keep.tile([P, T], U8, name="scale_table")
+        bias = keep.tile([P, HALVES], F32, name="bias")
+
+        nc.vector.memset(scale_table[:].bitcast(I32), 0)
+        nc.sync.dma_start(out=w_raw[:], in_=w.rearrange("(p j) m -> p j m", j=PACK))
+        nc.sync.dma_start(offsets[:], offs)
+        for q in range(4):
+            nc.scalar.dma_start(
+                out=scale_table[32 * q : 32 * q + 4, :].bitcast(I32),
+                in_=x_scales[0, 4 * q : 4 * q + 4, :].bitcast(I32),
+            )
+        nc.sync.dma_start(
+            out=word_table[:].bitcast(I32),
+            in_=x_words[0].rearrange("p n t -> p (n t)").bitcast(I32),
+        )
+        with nc.allow_non_contiguous_dma(reason="one bias value a partition"):
+            nc.sync.dma_start(out=bias[:], in_=b.rearrange("(h p) o -> p (h o)", p=P))
+
+        w_codes, w_scales = [], []
+        for h in range(HALVES):
+            grouped = keep.tile([P, P, PACK], BF16, name=f"w_grouped{h}", align_bytes=64)
+            src = w_raw[:, :, h * P : (h + 1) * P].rearrange("p j (c i) -> p c j i", i=4)
+            dst = grouped[:].rearrange("p (c i) j -> p c j i", i=4)
+            if h == 0:
+                nc.vector.tensor_copy(out=dst, in_=src)
+            else:
+                nc.scalar.copy(out=dst, in_=src)
+            codes = keep.tile([P, P], U32, name=f"w_codes{h}", align_bytes=64)
+            scales = keep.tile([P, P], U8, name=f"w_scales{h}", align_bytes=64)
+            nc.vector.quantize_mx(
+                out=codes[:].bitcast(FP8X4),
+                scales=scales[:],
+                in_=grouped[:].rearrange("p c j -> p (c j)"),
+            )
+            w_codes.append(codes)
+            w_scales.append(scales)
+
+        picked_scales = keep.tile([P, S], U8, name="picked_scales", align_bytes=64)
+        nc.vector.tensor_copy(picked_scales[:], scale_table[:].indirect(offsets[:]))
+
+        results = [keep.tile([P, V], F32, name=f"result{h}") for h in range(HALVES)]
+        picked = []
+        for c in range(CHUNKS):
+            words = keep.tile([P, CHUNK], U32, name=f"picked_words{c}", align_bytes=64)
+            cols = slice(c * CHUNK // LANES, (c + 1) * CHUNK // LANES)
+            nc.vector.tensor_copy(words[:], word_table[:].indirect(offsets[:, cols]))
+            picked.append(words)
+        for c in range(CHUNKS):
+            for h in range(HALVES):
+                acc = psum.tile([P, CHUNK], F32, name=f"acc{c}{h}")
+                nc.tensor.matmul_mx(
+                    out=acc[:],
+                    lhsT=w_codes[h][:].bitcast(FP8X4),
+                    lhsT_scale=w_scales[h][:],
+                    rhs=picked[c][:].bitcast(FP8X4),
+                    rhs_scale=picked_scales[:, c * CHUNK : (c + 1) * CHUNK],
+                    start=True,
+                    stop=True,
+                )
+                pooled = keep.tile([P, CHUNK // D], F32, name=f"pooled{c}{h}")
+                nc.vector.tensor_reduce(
+                    out=pooled[:], in_=acc[:].rearrange("p (v d) -> p v d", d=D), axis=AX_X, op=MAX
+                )
+                centres = slice(c * CHUNK // D, (c + 1) * CHUNK // D)
+                nc.scalar.activation(
+                    out=results[h][:, centres], in_=pooled[:], func=RELU, bias=bias[:, h : h + 1]
+                )
+        nc.sync.dma_start(out=out[0:P, :], in_=results[0][:])
+        nc.scalar.dma_start(out=out[P : 2 * P, :], in_=results[1][:])

@@ -40,7 +40,7 @@ def tile_picked_pool_lin_relu_sub_p_kernel(tc, x_words, x_scales, w, b, offs, ou
         nc.sync.dma_start(out=w_raw[:], in_=w.rearrange("(p j) m -> p j m", j=PACK))
         nc.sync.dma_start(offsets[:], offs)
         for q in range(4):
-            nc.scalar.dma_start(
+            nc.sync.dma_start(
                 out=scale_table[32 * q : 32 * q + 4, :].bitcast(I32),
                 in_=x_scales[0, 4 * q : 4 * q + 4, :].bitcast(I32),
             )

@@ -39,14 +39,18 @@ def tile_picked_pool_lin_relu_sub_p_kernel(tc, x_words, x_scales, w, b, offs, ou
         nc.vector.memset(scale_table[:].bitcast(I32), 0)
         nc.sync.dma_start(out=w_raw[:], in_=w.rearrange("(p j) m -> p j m", j=PACK))
         nc.sync.dma_start(offsets[:], offs)
-        for q in range(4):
+        nc.sync.dma_start(
+            out=word_table[:, 0:512].bitcast(I32),
+            in_=x_words[0].rearrange("p n t -> p (n t)").bitcast(I32)[:, 0:512],
+        )
+        for r in range(4):
             nc.sync.dma_start(
-                out=scale_table[32 * q : 32 * q + 4, :].bitcast(I32),
-                in_=x_scales[0, 4 * q : 4 * q + 4, :].bitcast(I32),
+                out=scale_table[r:P:32, :].bitcast(I32),
+                in_=x_scales[0, r:16:4, :].bitcast(I32),
             )
         nc.sync.dma_start(
-            out=word_table[:].bitcast(I32),
-            in_=x_words[0].rearrange("p n t -> p (n t)").bitcast(I32),
+            out=word_table[:, 512:2048].bitcast(I32),
+            in_=x_words[0].rearrange("p n t -> p (n t)").bitcast(I32)[:, 512:2048],
         )
         with nc.allow_non_contiguous_dma(reason="one bias value a partition"):
             nc.sync.dma_start(out=bias[:], in_=b.rearrange("(h p) o -> p (h o)", p=P))
@@ -101,4 +105,4 @@ def tile_picked_pool_lin_relu_sub_p_kernel(tc, x_words, x_scales, w, b, offs, ou
                     out=results[h][:, centres], in_=pooled[:], func=RELU, bias=bias[:, h : h + 1]
                 )
         nc.sync.dma_start(out=out[0:P, :], in_=results[0][:])
-        nc.scalar.dma_start(out=out[P : 2 * P, :], in_=results[1][:])
+        nc.sync.dma_start(out=out[P : 2 * P, :], in_=results[1][:])

@@ -18,10 +18,15 @@ AX_X = mybir.AxisListType.X
 
 P = 128
 PACK = 4
+BLOCKS = K // 32
+QUADRANT = 32
+QUADRANT_ROWS = 4
 HALVES = N // P
 CHUNK = 256
 CHUNKS = S // CHUNK
-LANES = 16
+LIST_ROWS = 16
+RUN = 4
+EARLY_COLUMNS = 256
 
 
 def tile_picked_pool_lin_relu_sub_p_kernel(tc, x_words, x_scales, w, b, offs, out):
@@ -30,40 +35,38 @@ def tile_picked_pool_lin_relu_sub_p_kernel(tc, x_words, x_scales, w, b, offs, ou
         keep = ctx.enter_context(tc.tile_pool(name="keep", bufs=1))
         psum = ctx.enter_context(tc.psum_pool(name="psum", bufs=1))
 
-        offsets = keep.tile([P, S // LANES], U16, name="offsets")
+        offsets = keep.tile([P, S // LIST_ROWS], U16, name="offsets")
         w_raw = keep.tile([P, PACK, N], F32, name="w_raw")
         word_table = keep.tile([P, T], U32, name="word_table")
         scale_table = keep.tile([P, T], U8, name="scale_table")
         bias = keep.tile([P, HALVES], F32, name="bias")
 
         nc.vector.memset(scale_table[:].bitcast(I32), 0)
+
         nc.sync.dma_start(out=w_raw[:], in_=w.rearrange("(p j) m -> p j m", j=PACK))
         nc.sync.dma_start(offsets[:], offs)
+        words_in = x_words[0].rearrange("p n t -> p (n t)").bitcast(I32)
         nc.sync.dma_start(
-            out=word_table[:, 0:512].bitcast(I32),
-            in_=x_words[0].rearrange("p n t -> p (n t)").bitcast(I32)[:, 0:512],
+            out=word_table[:, 0:EARLY_COLUMNS].bitcast(I32), in_=words_in[:, 0:EARLY_COLUMNS]
         )
-        for r in range(4):
+        for r in range(QUADRANT_ROWS):
             nc.sync.dma_start(
-                out=scale_table[r:P:32, :].bitcast(I32),
-                in_=x_scales[0, r:16:4, :].bitcast(I32),
+                out=scale_table[r:P:QUADRANT, :].bitcast(I32),
+                in_=x_scales[0, r:BLOCKS:QUADRANT_ROWS, :].bitcast(I32),
             )
         nc.sync.dma_start(
-            out=word_table[:, 512:2048].bitcast(I32),
-            in_=x_words[0].rearrange("p n t -> p (n t)").bitcast(I32)[:, 512:2048],
+            out=word_table[:, EARLY_COLUMNS:T].bitcast(I32), in_=words_in[:, EARLY_COLUMNS:T]
         )
         with nc.allow_non_contiguous_dma(reason="one bias value a partition"):
             nc.sync.dma_start(out=bias[:], in_=b.rearrange("(h p) o -> p (h o)", p=P))
 
         w_codes, w_scales = [], []
-        for h in range(HALVES):
+        for h, copy in enumerate((nc.vector.tensor_copy, nc.scalar.copy)):
             grouped = keep.tile([P, P, PACK], BF16, name=f"w_grouped{h}", align_bytes=64)
-            src = w_raw[:, :, h * P : (h + 1) * P].rearrange("p j (c i) -> p c j i", i=4)
-            dst = grouped[:].rearrange("p (c i) j -> p c j i", i=4)
-            if h == 0:
-                nc.vector.tensor_copy(out=dst, in_=src)
-            else:
-                nc.scalar.copy(out=dst, in_=src)
+            copy(
+                out=grouped[:].rearrange("p (c i) j -> p c j i", i=RUN),
+                in_=w_raw[:, :, h * P : (h + 1) * P].rearrange("p j (c i) -> p c j i", i=RUN),
+            )
             codes = keep.tile([P, P], U32, name=f"w_codes{h}", align_bytes=64)
             scales = keep.tile([P, P], U8, name=f"w_scales{h}", align_bytes=64)
             nc.vector.quantize_mx(
@@ -78,12 +81,13 @@ def tile_picked_pool_lin_relu_sub_p_kernel(tc, x_words, x_scales, w, b, offs, ou
         nc.vector.tensor_copy(picked_scales[:], scale_table[:].indirect(offsets[:]))
 
         results = [keep.tile([P, V], F32, name=f"result{h}") for h in range(HALVES)]
-        picked = []
+        picked_words = []
         for c in range(CHUNKS):
             words = keep.tile([P, CHUNK], U32, name=f"picked_words{c}", align_bytes=64)
-            cols = slice(c * CHUNK // LANES, (c + 1) * CHUNK // LANES)
-            nc.vector.tensor_copy(words[:], word_table[:].indirect(offsets[:, cols]))
-            picked.append(words)
+            list_columns = slice(c * CHUNK // LIST_ROWS, (c + 1) * CHUNK // LIST_ROWS)
+            nc.vector.tensor_copy(words[:], word_table[:].indirect(offsets[:, list_columns]))
+            picked_words.append(words)
+
         for c in range(CHUNKS):
             for h in range(HALVES):
                 acc = psum.tile([P, CHUNK], F32, name=f"acc{c}{h}")
@@ -91,7 +95,7 @@ def tile_picked_pool_lin_relu_sub_p_kernel(tc, x_words, x_scales, w, b, offs, ou
                     out=acc[:],
                     lhsT=w_codes[h][:].bitcast(FP8X4),
                     lhsT_scale=w_scales[h][:],
-                    rhs=picked[c][:].bitcast(FP8X4),
+                    rhs=picked_words[c][:].bitcast(FP8X4),
                     rhs_scale=picked_scales[:, c * CHUNK : (c + 1) * CHUNK],
                     start=True,
                     stop=True,
@@ -104,5 +108,6 @@ def tile_picked_pool_lin_relu_sub_p_kernel(tc, x_words, x_scales, w, b, offs, ou
                 nc.scalar.activation(
                     out=results[h][:, centres], in_=pooled[:], func=RELU, bias=bias[:, h : h + 1]
                 )
-        nc.sync.dma_start(out=out[0:P, :], in_=results[0][:])
-        nc.sync.dma_start(out=out[P : 2 * P, :], in_=results[1][:])
+
+        for h in range(HALVES):
+            nc.sync.dma_start(out=out[h * P : (h + 1) * P, :], in_=results[h][:])

@@ -14,6 +14,7 @@ U8 = mybir.dt.uint8
 FP8X4 = mybir.dt.float8_e4m3fn_x4
 RELU = mybir.ActivationFunctionType.Relu
 MAX = mybir.AluOpType.max
+ADD = mybir.AluOpType.add
 AX_X = mybir.AxisListType.X
 
 P = 128
@@ -80,7 +81,6 @@ def tile_picked_pool_lin_relu_sub_p_kernel(tc, x_words, x_scales, w, b, offs, ou
         picked_scales = keep.tile([P, S], U8, name="picked_scales", align_bytes=64)
         nc.vector.tensor_copy(picked_scales[:], scale_table[:].indirect(offsets[:]))
 
-        results = [keep.tile([P, V], F32, name=f"result{h}") for h in range(HALVES)]
         picked_words = []
         for c in range(CHUNKS):
             words = keep.tile([P, CHUNK], U32, name=f"picked_words{c}", align_bytes=64)
@@ -104,10 +104,19 @@ def tile_picked_pool_lin_relu_sub_p_kernel(tc, x_words, x_scales, w, b, offs, ou
                 nc.vector.tensor_reduce(
                     out=pooled[:], in_=acc[:].rearrange("p (v d) -> p v d", d=D), axis=AX_X, op=MAX
                 )
+                result = keep.tile([P, CHUNK // D], F32, name=f"result{c}{h}")
+                if (c, h) == (CHUNKS - 1, HALVES - 1):
+                    nc.vector.tensor_scalar(
+                        out=result[:],
+                        in0=pooled[:],
+                        scalar1=bias[:, h : h + 1],
+                        scalar2=0.0,
+                        op0=ADD,
+                        op1=MAX,
+                    )
+                else:
+                    nc.scalar.activation(
+                        out=result[:], in_=pooled[:], func=RELU, bias=bias[:, h : h + 1]
+                    )
                 centres = slice(c * CHUNK // D, (c + 1) * CHUNK // D)
-                nc.scalar.activation(
-                    out=results[h][:, centres], in_=pooled[:], func=RELU, bias=bias[:, h : h + 1]
-                )
-
-        for h in range(HALVES):
-            nc.sync.dma_start(out=out[h * P : (h + 1) * P, :], in_=results[h][:])
+                nc.sync.dma_start(out=out[h * P : (h + 1) * P, centres], in_=result[:])

from contextlib import ExitStack

import concourse.mybir as mybir

K, T, D, S, V, N = 512, 2048, 4, 512, 128, 256
FLOPS = 2 * K * N * S

F32 = mybir.dt.float32
BF16 = mybir.dt.bfloat16
I32 = mybir.dt.int32
U32 = mybir.dt.uint32
U16 = mybir.dt.uint16
U8 = mybir.dt.uint8
FP8X4 = mybir.dt.float8_e4m3fn_x4
RELU = mybir.ActivationFunctionType.Relu
MAX = mybir.AluOpType.max
ADD = mybir.AluOpType.add
AX_X = mybir.AxisListType.X

P = 128
PACK = 4
BLOCKS = K // 32
QUADRANT = 32
QUADRANT_ROWS = 4
HALVES = N // P
CHUNK = 256
CHUNKS = S // CHUNK
LIST_ROWS = 16
RUN = 4
EARLY_COLUMNS = 256


def tile_picked_pool_lin_relu_sub_p_kernel(tc, x_words, x_scales, w, b, offs, out):
    nc = tc.nc
    with ExitStack() as ctx:
        keep = ctx.enter_context(tc.tile_pool(name="keep", bufs=1))
        psum = ctx.enter_context(tc.psum_pool(name="psum", bufs=1))

        offsets = keep.tile([P, S // LIST_ROWS], U16, name="offsets")
        w_raw = keep.tile([P, PACK, N], F32, name="w_raw")
        word_table = keep.tile([P, T], U32, name="word_table")
        scale_table = keep.tile([P, T], U8, name="scale_table")
        bias = keep.tile([P, HALVES], F32, name="bias")

        nc.vector.memset(scale_table[:].bitcast(I32), 0)

        nc.sync.dma_start(out=w_raw[:], in_=w.rearrange("(p j) m -> p j m", j=PACK))
        nc.sync.dma_start(offsets[:], offs)
        words_in = x_words[0].rearrange("p n t -> p (n t)").bitcast(I32)
        nc.sync.dma_start(
            out=word_table[:, 0:EARLY_COLUMNS].bitcast(I32), in_=words_in[:, 0:EARLY_COLUMNS]
        )
        for r in range(QUADRANT_ROWS):
            nc.sync.dma_start(
                out=scale_table[r:P:QUADRANT, :].bitcast(I32),
                in_=x_scales[0, r:BLOCKS:QUADRANT_ROWS, :].bitcast(I32),
            )
        nc.sync.dma_start(
            out=word_table[:, EARLY_COLUMNS:T].bitcast(I32), in_=words_in[:, EARLY_COLUMNS:T]
        )
        with nc.allow_non_contiguous_dma(reason="one bias value a partition"):
            nc.sync.dma_start(out=bias[:], in_=b.rearrange("(h p) o -> p (h o)", p=P))

        w_codes, w_scales = [], []
        for h, copy in enumerate((nc.vector.tensor_copy, nc.scalar.copy)):
            grouped = keep.tile([P, P, PACK], BF16, name=f"w_grouped{h}", align_bytes=64)
            copy(
                out=grouped[:].rearrange("p (c i) j -> p c j i", i=RUN),
                in_=w_raw[:, :, h * P : (h + 1) * P].rearrange("p j (c i) -> p c j i", i=RUN),
            )
            codes = keep.tile([P, P], U32, name=f"w_codes{h}", align_bytes=64)
            scales = keep.tile([P, P], U8, name=f"w_scales{h}", align_bytes=64)
            nc.vector.quantize_mx(
                out=codes[:].bitcast(FP8X4),
                scales=scales[:],
                in_=grouped[:].rearrange("p c j -> p (c j)"),
            )
            w_codes.append(codes)
            w_scales.append(scales)

        picked_scales = keep.tile([P, S], U8, name="picked_scales", align_bytes=64)
        nc.vector.tensor_copy(picked_scales[:], scale_table[:].indirect(offsets[:]))

        picked_words = []
        for c in range(CHUNKS):
            words = keep.tile([P, CHUNK], U32, name=f"picked_words{c}", align_bytes=64)
            list_columns = slice(c * CHUNK // LIST_ROWS, (c + 1) * CHUNK // LIST_ROWS)
            nc.vector.tensor_copy(words[:], word_table[:].indirect(offsets[:, list_columns]))
            picked_words.append(words)

        for c in range(CHUNKS):
            for h in range(HALVES):
                acc = psum.tile([P, CHUNK], F32, name=f"acc{c}{h}")
                nc.tensor.matmul_mx(
                    out=acc[:],
                    lhsT=w_codes[h][:].bitcast(FP8X4),
                    lhsT_scale=w_scales[h][:],
                    rhs=picked_words[c][:].bitcast(FP8X4),
                    rhs_scale=picked_scales[:, c * CHUNK : (c + 1) * CHUNK],
                    start=True,
                    stop=True,
                )
                pooled = keep.tile([P, CHUNK // D], F32, name=f"pooled{c}{h}")
                nc.vector.tensor_reduce(
                    out=pooled[:], in_=acc[:].rearrange("p (v d) -> p v d", d=D), axis=AX_X, op=MAX
                )
                result = keep.tile([P, CHUNK // D], F32, name=f"result{c}{h}")
                if (c, h) == (CHUNKS - 1, HALVES - 1):
                    nc.vector.tensor_scalar(
                        out=result[:],
                        in0=pooled[:],
                        scalar1=bias[:, h : h + 1],
                        scalar2=0.0,
                        op0=ADD,
                        op1=MAX,
                    )
                else:
                    nc.scalar.activation(
                        out=result[:], in_=pooled[:], func=RELU, bias=bias[:, h : h + 1]
                    )
                centres = slice(c * CHUNK // D, (c + 1) * CHUNK // D)
                nc.sync.dma_start(out=out[h * P : (h + 1) * P, centres], in_=result[:])
